import numpy as np
import ml_dtypes


def mxq(x, axis, fmt="e4m3"):
    dtype, down = {"e4m3": (ml_dtypes.float8_e4m3fn, 7), "e5m2": (ml_dtypes.float8_e5m2, 14)}[fmt]
    v = np.moveaxis(np.asarray(x, np.float32).astype(ml_dtypes.bfloat16).astype(np.float64), axis, -1)
    blocks = v.reshape(v.shape[:-1] + (-1, 32))
    amax = np.abs(blocks).max(-1, keepdims=True)
    byte = np.maximum(np.where(amax > 0, np.frexp(amax)[1] - 1 + 127, 0) - down, 1)
    scale = np.exp2(byte - 127.0)
    codes = (blocks / scale).astype(np.float32).astype(dtype).astype(np.float64)
    return np.moveaxis((codes * scale).reshape(v.shape), -1, axis)


WIDE = False


def mx_kscale(k):
    if not WIDE:
        return np.ones(k)
    levels = np.array([10, -10, 5, -5, 0])
    if k % 512:
        return np.exp2(np.random.permutation(np.resize(levels, k // 32))).repeat(32)
    a = np.empty((k // 512, 16))
    for p in range(k // 512):
        a[p, :8] = np.random.permutation(np.resize(levels, 8))
        for g in range(8):
            far = levels[np.abs(levels - a[p, g]) >= 10]
            a[p, g + 8] = far[np.random.randint(len(far))]
    return np.exp2(a.ravel()).repeat(32)


def f64(x):
    return np.asarray(x).astype(np.float64)


def striped(idx):
    return np.tile(idx.reshape(-1, 16).T, (8, 1)).astype(np.uint16)


def unstriped(offs):
    return offs[:16].T.reshape(-1).astype(np.int64)


def pack_weight(w):
    k, n = w.shape
    w = f64(np.asarray(w, np.float32).astype(ml_dtypes.bfloat16)).reshape(k // 32, 32, n)
    amax = np.abs(w).max(1)
    byte = np.clip(np.where(amax > 0, np.frexp(amax)[1] - 1 + 127 - 7, 1), 1, 254)
    scaled = (w * np.exp2(127.0 - byte)[:, None, :]).reshape(k, n).astype(np.float32)
    words = np.ascontiguousarray(scaled.reshape(k // 512, 128, 4, n).transpose(0, 1, 3, 2)).astype(ml_dtypes.float8_e4m3fn).view(np.uint8)
    return words, np.ascontiguousarray(byte.astype(np.uint8).reshape(k // 512, 16, n))


def unpack_weight(words, scales):
    g, p, n, _ = words.shape
    vals = np.ascontiguousarray(words).view(ml_dtypes.float8_e4m3fn).astype(np.float64) * np.repeat(np.exp2(scales.astype(np.float64) - 127.0), 8, axis=1)[..., None]
    return vals.transpose(0, 1, 3, 2).reshape(g * 512, n)


def relu(v):
    return np.maximum(v, 0.0)


K, T, S, N, D, V = 1024, 2048, 512, 128, 4, 256
P = 2 ** 7


def setup_inputs():
    n = np.random.standard_normal
    s = mx_kscale(K)[:, None]
    packed_xT = pack_weight(n((K, T)) * s)
    return {
        "x_words": packed_xT[0],
        "x_scales": packed_xT[1],
        "w1": (n((K, N)) / np.sqrt(K) / s).astype(np.float32),
        "w2": (n((K, N)) / np.sqrt(K) / s).astype(np.float32),
        "w3": (n((K, N)) / np.sqrt(K) / s).astype(np.float32),
        "tri": (np.tile(np.random.uniform(0.1, 0.6, (D, 1, V)), (1, P, 1))).astype(np.float32),
        "dist": (np.tile(np.random.uniform(0.2, 1.5, (D, 1, V)), (1, P, 1))).astype(np.float32),
        "offs": striped(np.random.permutation(T)[:S]),
        "pos1": striped(np.random.permutation(S)[:V]),
        "pos2": striped(np.random.permutation(S)[:V]),
        "pos3": striped(np.random.permutation(S)[:V]),
        "pos4": striped(np.random.permutation(S)[:V]),
    }


def reference(x_words, x_scales, w1, w2, w3, tri, dist, offs, pos1, pos2, pos3, pos4):
    xq = unpack_weight(x_words, x_scales)[:, unstriped(offs)]
    mean = mxq(f64(w2), 0, "e4m3").T @ xq
    mu = np.log(np.exp(mean) + 1.0)
    msq = mxq(f64(w3), 0, "e4m3").T @ xq
    var = np.abs((mu) ** 2 - (np.log(np.exp(msq) + 1.0))) + 0.05
    ch0 = f64(tri)[0, :1] * (var[:, unstriped(pos1)] / (var[:, unstriped(pos1)] + (relu(f64(dist)[0, :1] - mu[:, unstriped(pos1)])) ** 2))
    irr = mxq(f64(w1), 0, "e4m3").T @ xq
    er = np.exp(0.5 * irr)
    ch1 = f64(tri)[1, :1] * (var[:, unstriped(pos2)] / (var[:, unstriped(pos2)] + (relu(f64(dist)[1, :1] - mu[:, unstriped(pos2)])) ** 2))
    ch2 = f64(tri)[2, :1] * (var[:, unstriped(pos3)] / (var[:, unstriped(pos3)] + (relu(f64(dist)[2, :1] - mu[:, unstriped(pos3)])) ** 2))
    ch3 = f64(tri)[3, :1] * (var[:, unstriped(pos4)] / (var[:, unstriped(pos4)] + (relu(f64(dist)[3, :1] - mu[:, unstriped(pos4)])) ** 2))
    return np.sqrt((ch0 * er[:, unstriped(pos1)] + ch1 * er[:, unstriped(pos2)] + ch2 * er[:, unstriped(pos3)] + ch3 * er[:, unstriped(pos4)]) / (ch0 + ch1 + ch2 + ch3 + 0.02))

@@ -1,0 +1,204 @@
+from contextlib import ExitStack
+
+import concourse.mybir as mybir
+from concourse.masks import make_identity
+
+K, T, S, M, D, V = 1024, 2048, 512, 128, 4, 256
+FLOPS = 3 * 2 * K * M * S
+
+F32 = mybir.dt.float32
+BF16 = mybir.dt.bfloat16
+I32 = mybir.dt.int32
+U32 = mybir.dt.uint32
+U16 = mybir.dt.uint16
+U8 = mybir.dt.uint8
+FP8X4 = mybir.dt.float8_e4m3fn_x4
+ALU = mybir.AluOpType
+ACT = mybir.ActivationFunctionType
+
+P = 128
+PACK = 4
+PASSES = K // (P * PACK)
+EXP_CAP = 2.0 ** 60
+TINY = 1e-30
+H = V // P
+
+
+def tile_picked_yddgi_root_p_kernel(
+    tc, x_words, x_scales, w1, w2, w3, tri, dist, offs, pos1, pos2, pos3, pos4, out
+):
+    nc = tc.nc
+    with ExitStack() as ctx:
+        held = ctx.enter_context(tc.tile_pool(name="held", bufs=1))
+        psum = ctx.enter_context(tc.psum_pool(name="psum", bufs=1))
+
+        def row(name, width=S):
+            return held.tile([P, width], F32, name=name)
+
+        def bank(name, b, shape):
+            return psum.tile(shape, F32, name=name, tag="bank%d" % b)
+
+        offs_t = held.tile([P, S // 16], U16, name="offs_t")
+        pos_t = [held.tile([P, V // 16], U16, name="pos_t%d" % d) for d in range(D)]
+        x_tab = [held.tile([P, T], U32, name="x_tab%d" % o) for o in range(PASSES)]
+        s_tab = held.tile([P, T], U8, name="s_tab")
+        w_raw = [[held.tile([P, PACK, M], F32, name="w_raw%d_%d" % (i, o)) for o in range(PASSES)] for i in range(3)]
+        ident = row("ident", P)
+        tri_rows, dist_rows = row("tri_rows", P), row("dist_rows", P)
+
+        nc.vector.memset(s_tab[:].bitcast(I32), 0)
+        make_identity(nc, ident[:])
+
+        nc.sync.dma_start(offs_t[:], offs)
+        nc.sync.dma_start(x_tab[0][:].bitcast(I32), x_words[0].rearrange("p n t -> p (n t)").bitcast(I32))
+        for q in range(4):
+            nc.sync.dma_start(s_tab[32 * q : 32 * q + 4 * PASSES, :].bitcast(I32), x_scales[:, 4 * q : 4 * q + 4, :].bitcast(I32))
+
+        def load_weights(i, o):
+            rows = (w1, w2, w3)[i][o * P * PACK : (o + 1) * P * PACK, :]
+            nc.sync.dma_start(w_raw[i][o][:], rows.rearrange("(p t) m -> p t m", t=PACK))
+
+        for i in range(3):
+            load_weights(i, 0)
+        nc.sync.dma_start(x_tab[1][:].bitcast(I32), x_words[1].rearrange("p n t -> p (n t)").bitcast(I32))
+        for i in range(3):
+            load_weights(i, 1)
+        for d, pos in enumerate((pos1, pos2, pos3, pos4)):
+            nc.sync.dma_start(pos_t[d][:], pos)
+        for rows, src in ((tri_rows, tri), (dist_rows, dist)):
+            nc.sync.dma_start(rows[:], src[:, 0 : P // (D * H), :].rearrange("d r (h v) -> d (r h) v", h=H))
+
+        x_pick = [held.tile([P, S], U32, name="x_pick%d" % o, align_bytes=64) for o in range(PASSES)]
+        s_pick = held.tile([P, S], U8, name="s_pick", align_bytes=64)
+        nc.vector.tensor_copy(x_pick[0][:], x_tab[0][:].indirect(offs_t[:]))
+        nc.vector.tensor_copy(s_pick[:], s_tab[:].indirect(offs_t[:]))
+        nc.vector.tensor_copy(x_pick[1][:], x_tab[1][:].indirect(offs_t[:]))
+
+        acc = [bank("product%d" % i, i, [P, S]) for i in range(3)]
+        for o in range(PASSES):
+            for i in range(3):
+                product = acc[i]
+                w_bf = held.tile([P, M, PACK], BF16, name="w_bf%d_%d" % (i, o), align_bytes=64)
+                w_codes = held.tile([P, M], U32, name="w_codes%d_%d" % (i, o), align_bytes=64)
+                w_scales = held.tile([P, M], U8, name="w_scales%d_%d" % (i, o), align_bytes=64)
+                src = w_raw[i][o][:].rearrange("p t m -> p m t")
+                if (i, o) != (2, 1):
+                    nc.scalar.copy(w_bf[:], src)
+                else:
+                    nc.vector.tensor_copy(w_bf[:], src)
+                nc.vector.quantize_mx(
+                    out=w_codes[:].bitcast(FP8X4), scales=w_scales[:], in_=w_bf[:].rearrange("p m t -> p (m t)")
+                )
+                nc.tensor.matmul_mx(
+                    out=product[:],
+                    lhsT=w_codes[:].bitcast(FP8X4),
+                    lhsT_scale=w_scales[:],
+                    rhs=x_pick[o][:].bitcast(FP8X4),
+                    rhs_scale=s_pick[4 * o : P, :],
+                    start=(o == 0),
+                    stop=(o == PASSES - 1),
+                )
+        irr, mean, msq = acc
+
+        def fetch_turned(picked, window, d, dst):
+            nc.vector.tensor_copy(picked, window[:].indirect(pos_t[d][:]))
+            for h in range(H):
+                nc.tensor.transpose(dst[:, h, :], picked[:, h * P : (h + 1) * P], ident[:])
+
+        er = row("er")
+        grown = held.tile([P, 2, S], F32, name="grown")
+        capped = held.tile([P, 2, S], F32, name="capped")
+        nc.scalar.activation(er[:], irr[:], ACT.Exp, scale=0.5)
+        nc.scalar.activation(grown[:, 0, :], mean[:], ACT.Exp)
+        nc.scalar.activation(grown[:, 1, :], msq[:], ACT.Exp)
+        nc.vector.tensor_scalar(capped[:], grown[:], EXP_CAP, None, ALU.min)
+
+        turned = bank("turned", 7, [P, 2, D, P // D])
+        nc.tensor.transpose(turned[:, 0].rearrange("p d c -> p (d c)"), tri_rows[:], ident[:])
+        nc.tensor.transpose(turned[:, 1].rearrange("p d c -> p (d c)"), dist_rows[:], ident[:])
+        cols = held.tile([P, 2, D, H], F32, name="cols")
+        nc.vector.tensor_copy(cols[:], turned[:, :, :, 0:H])
+        tri_col, dist_col = cols[:, 0], cols[:, 1]
+
+        er_pair = [bank("er_pair%d" % a, 3 + a, [P, 2, H, P]) for a in range(D // 2)]
+        er_t = [er_pair[d // 2][:, d % 2] for d in range(D)]
+        er_pick = [
+            held.tile([P, 2, V], F32, name="er_early", tag="w_bf2_1", align_bytes=64),
+            held.tile([P, 2, V], F32, name="er_late", tag="grown"),
+        ]
+        for d in range(D):
+            fetch_turned(er_pick[d // 2][:, d % 2, :], er, d, er_t[d])
+
+        log_mean, log_msq, mu, sq = row("log_mean"), row("log_msq"), row("mu"), row("sq")
+        nc.scalar.activation(log_mean[:], capped[:, 0, :], ACT.Ln, bias=1.0)
+        nc.scalar.activation(log_msq[:], capped[:, 1, :], ACT.Ln, bias=1.0)
+        nc.vector.tensor_tensor(mu[:], mean[:], log_mean[:], ALU.max)
+        nc.vector.tensor_tensor(sq[:], msq[:], log_msq[:], ALU.max)
+
+        mu2, diff, spread, rstd = row("mu2"), row("diff"), row("spread"), row("rstd")
+        nc.vector.tensor_tensor(mu2[:], mu[:], mu[:], ALU.mult)
+        r_tri = held.tile([P, D, H], F32, name="r_tri", tag="log_mean")
+        root_tri = held.tile([P, D, H], F32, name="root_tri")
+        nc.scalar.activation(r_tri[:], tri_col, ACT.Abs_reciprocal_sqrt, bias=TINY)
+        nc.vector.tensor_tensor(diff[:], mu2[:], sq[:], ALU.subtract)
+        nc.scalar.activation(spread[:], diff[:], ACT.Abs)
+        nc.scalar.activation(rstd[:], spread[:], ACT.Abs_reciprocal_sqrt, bias=0.05)
+        inv_var = row("inv_var")
+        nc.scalar.activation(inv_var[:], rstd[:], ACT.Square)
+        nc.vector.tensor_tensor(root_tri[:], tri_col, r_tri[:], ALU.mult)
+
+        mu_picks = held.tile([P, D, V], F32, name="mu_picks", tag="mu2")
+        mu_pick = [mu_picks[:, d, :] for d in range(D)]
+        gap = []
+        for d in range(D):
+            mu_t = bank("mu_t%d" % d, (5, 6, 1, 2)[d], [P, H, P])
+            fetch_turned(mu_pick[d], mu, d, mu_t)
+            g = held.tile([P, H, P], F32, name="gap%d" % d)
+            for h in range(H):
+                nc.scalar.activation(g[:, h, :], mu_t[:, h, :], ACT.Relu, scale=-1.0, bias=dist_col[:, d, h : h + 1])
+            g2 = held.tile([P, H, P], F32, name="gap_sq%d" % d)
+            nc.scalar.activation(g2[:], g[:], ACT.Square)
+            gap.append(g2)
+
+        rstd_t = []
+        for d in range(D):
+            dst = bank("rstd_t%d" % d, (0, 7)[d % 2], [P, H, P])
+            rstd_t.append(dst)
+        den = [bank("den%d" % h, 1 + h, [P, P]) for h in range(H)]
+        num = [bank("num%d" % h, 5 + h, [P, P]) for h in range(H)]
+
+        def fetch_rstd(d):
+            tag = "rstd_pick%d" % d if d < 2 else "gap_sq%d" % (d - 2)
+            picked = held.tile([P, V], F32, name="rstd_pick%d" % d, tag=tag)
+            fetch_turned(picked[:], inv_var, d, rstd_t[d])
+
+        fetch_rstd(0)
+        for d in range(D):
+            if d + 1 < D:
+                fetch_rstd(d + 1)
+            ratio = held.tile([P, H, P], F32, name="ratio%d" % d)
+            root = held.tile([P, H, P], F32, name="root%d" % d, tag="gap%d" % (D - 1 - d))
+            weight = held.tile([P, H, P], F32, name="weight%d" % d)
+            term = held.tile([P, H, P], F32, name="term%d" % d)
+            nc.vector.tensor_tensor(ratio[:], rstd_t[d][:], gap[d][:], ALU.mult)
+            nc.scalar.activation(root[:], ratio[:], ACT.Abs_reciprocal_sqrt, bias=1.0)
+            for h in range(H):
+                nc.scalar.activation(weight[:, h, :], root[:, h, :], ACT.Square, scale=root_tri[:, d, h : h + 1])
+            nc.vector.tensor_tensor(term[:], er_t[d], weight[:], ALU.mult)
+            for total, part in ((den, weight), (num, term)):
+                for h in range(H):
+                    nc.tensor.matmul(total[h][:], part[:, h, :], ident[:], start=(d == 0), stop=(d == D - 1), is_transpose=True)
+
+        res = row("res", V)
+        r_den = [row("r_den%d" % h, P) for h in range(H)]
+        for h in range(H):
+            nc.scalar.activation(r_den[h][:], den[h][:], ACT.Abs_reciprocal_sqrt, bias=0.02)
+        for h in range(H):
+            r_num, part = row("r_num%d" % h, P), row("part%d" % h, P)
+            if h == 0:
+                nc.vector.tensor_tensor(part[:], num[h][:], r_den[h][:], ALU.mult)
+            nc.scalar.activation(r_num[:], num[h][:], ACT.Abs_reciprocal_sqrt, bias=TINY)
+            if h == 1:
+                nc.vector.tensor_tensor(part[:], num[h][:], r_den[h][:], ALU.mult)
+            nc.vector.tensor_tensor(res[:, h * P : (h + 1) * P], part[:], r_num[:], ALU.mult)
+        nc.sync.dma_start(out, res[:])

@@ -46,13 +46,13 @@ def tile_picked_yddgi_root_p_kernel(
         ident = row("ident", P)
         tri_rows, dist_rows = row("tri_rows", P), row("dist_rows", P)
 
-        nc.vector.memset(s_tab[:].bitcast(I32), 0)
+        nc.gpsimd.memset(s_tab[:].bitcast(I32), 0)
+        for q in range(4):
+            nc.gpsimd.dma_start(s_tab[32 * q : 32 * q + 4 * PASSES, :].bitcast(I32), x_scales[:, 4 * q : 4 * q + 4, :].bitcast(I32))
         make_identity(nc, ident[:])
 
         nc.sync.dma_start(offs_t[:], offs)
         nc.sync.dma_start(x_tab[0][:].bitcast(I32), x_words[0].rearrange("p n t -> p (n t)").bitcast(I32))
-        for q in range(4):
-            nc.sync.dma_start(s_tab[32 * q : 32 * q + 4 * PASSES, :].bitcast(I32), x_scales[:, 4 * q : 4 * q + 4, :].bitcast(I32))
 
         def load_weights(i, o):
             rows = (w1, w2, w3)[i][o * P * PACK : (o + 1) * P * PACK, :]
@@ -123,11 +123,11 @@ def tile_picked_yddgi_root_p_kernel(
         er_pair = [bank("er_pair%d" % a, 3 + a, [P, 2, H, P]) for a in range(D // 2)]
         er_t = [er_pair[d // 2][:, d % 2] for d in range(D)]
         er_pick = [
-            held.tile([P, 2, V], F32, name="er_early", tag="w_bf2_1", align_bytes=64),
-            held.tile([P, 2, V], F32, name="er_late", tag="grown"),
+            held.tile([P, D - 1, V], F32, name="er_early", tag="w_bf2_1", align_bytes=64),
+            held.tile([P, 1, V], F32, name="er_late", tag="grown"),
         ]
         for d in range(D):
-            fetch_turned(er_pick[d // 2][:, d % 2, :], er, d, er_t[d])
+            fetch_turned(er_pick[d // (D - 1)][:, d % (D - 1), :], er, d, er_t[d])
 
         log_mean, log_msq, mu, sq = row("log_mean"), row("log_msq"), row("mu"), row("sq")
         nc.scalar.activation(log_mean[:], capped[:, 0, :], ACT.Ln, bias=1.0)
@@ -149,45 +149,57 @@ def tile_picked_yddgi_root_p_kernel(
 
         mu_picks = held.tile([P, D, V], F32, name="mu_picks", tag="mu2")
         mu_pick = [mu_picks[:, d, :] for d in range(D)]
-        gap = []
+        first_gap = held.tile([P, H, P], F32, name="first_gap", tag="spread")
+        later_gaps = held.tile([P, D - 1, H, P], F32, name="later_gaps", tag="rstd")
+        gap = [first_gap[:]] + [later_gaps[:, d] for d in range(D - 1)]
+        gap_sq = [held.tile([P, H, P], F32, name="gap_sq%d" % d) for d in range(D)]
         for d in range(D):
             mu_t = bank("mu_t%d" % d, (5, 6, 1, 2)[d], [P, H, P])
             fetch_turned(mu_pick[d], mu, d, mu_t)
-            g = held.tile([P, H, P], F32, name="gap%d" % d)
             for h in range(H):
-                nc.scalar.activation(g[:, h, :], mu_t[:, h, :], ACT.Relu, scale=-1.0, bias=dist_col[:, d, h : h + 1])
-            g2 = held.tile([P, H, P], F32, name="gap_sq%d" % d)
-            nc.scalar.activation(g2[:], g[:], ACT.Square)
-            gap.append(g2)
+                nc.scalar.activation(gap[d][:, h, :], mu_t[:, h, :], ACT.Relu, scale=-1.0, bias=dist_col[:, d, h : h + 1])
+            if d > 0:
+                nc.scalar.activation(gap_sq[d - 1][:], gap[d - 1], ACT.Square)
+        nc.scalar.activation(gap_sq[D - 1][:], gap[D - 1], ACT.Square)
 
-        rstd_t = []
-        for d in range(D):
-            dst = bank("rstd_t%d" % d, (0, 7)[d % 2], [P, H, P])
-            rstd_t.append(dst)
-        den = [bank("den%d" % h, 1 + h, [P, P]) for h in range(H)]
-        num = [bank("num%d" % h, 5 + h, [P, P]) for h in range(H)]
+        steps = [(d, 0, H) for d in range(D - 1)] + [(D - 1, h, h + 1) for h in range(H)]
+        root = held.tile([P, D, H, P], F32, name="root", tag="rstd")
+        ratio = held.tile([P, D, H, P], F32, name="ratio")
+        weight = held.tile([P, D, H, P], F32, name="weight")
+        term = held.tile([P, D, H, P], F32, name="term", tag="gap_sq%d" % (D - 1))
+        inv_t = []
 
-        def fetch_rstd(d):
-            tag = "rstd_pick%d" % d if d < 2 else "gap_sq%d" % (d - 2)
-            picked = held.tile([P, V], F32, name="rstd_pick%d" % d, tag=tag)
-            fetch_turned(picked[:], inv_var, d, rstd_t[d])
+        def fetch_inv_var(s):
+            d, h0, h1 = steps[s]
+            picked = held.tile([P, h1 - h0, P], F32, name="inv_pick%d" % s)
+            dst = bank("inv_t%d" % s, (0, 7, 5, 6, 1)[s], [P, h1 - h0, P])
+            cols16 = P // 16
+            nc.vector.tensor_copy(
+                picked[:].rearrange("p h v -> p (h v)"), inv_var[:].indirect(pos_t[d][:, h0 * cols16 : h1 * cols16])
+            )
+            for h in range(h1 - h0):
+                nc.tensor.transpose(dst[:, h, :], picked[:, h, :], ident[:])
+            inv_t.append(dst)
 
-        fetch_rstd(0)
-        for d in range(D):
-            if d + 1 < D:
-                fetch_rstd(d + 1)
-            ratio = held.tile([P, H, P], F32, name="ratio%d" % d)
-            root = held.tile([P, H, P], F32, name="root%d" % d, tag="gap%d" % (D - 1 - d))
-            weight = held.tile([P, H, P], F32, name="weight%d" % d)
-            term = held.tile([P, H, P], F32, name="term%d" % d)
-            nc.vector.tensor_tensor(ratio[:], rstd_t[d][:], gap[d][:], ALU.mult)
-            nc.scalar.activation(root[:], ratio[:], ACT.Abs_reciprocal_sqrt, bias=1.0)
-            for h in range(H):
-                nc.scalar.activation(weight[:, h, :], root[:, h, :], ACT.Square, scale=root_tri[:, d, h : h + 1])
-            nc.vector.tensor_tensor(term[:], er_t[d], weight[:], ALU.mult)
+        for s in range(len(steps)):
+            fetch_inv_var(s)
+        for s, (d, h0, h1) in enumerate(steps):
+            nc.vector.tensor_tensor(ratio[:, d, h0:h1], inv_t[s][:], gap_sq[d][:, h0:h1], ALU.mult)
+        den = [bank("den%d" % h, (2, 0)[h], [P, P]) for h in range(H)]
+        num = [bank("num%d" % h, (7, 5)[h], [P, P]) for h in range(H)]
+        for d, h0, h1 in steps:
+            nc.scalar.activation(root[:, d, h0:h1], ratio[:, d, h0:h1], ACT.Abs_reciprocal_sqrt, bias=1.0)
+            for h in range(h0, h1):
+                if d % 2 == 0:
+                    nc.vector.scalar_tensor_tensor(
+                        weight[:, d, h], root[:, d, h], tri_col[:, d, h : h + 1], root[:, d, h], ALU.mult, ALU.mult
+                    )
+                else:
+                    nc.scalar.activation(weight[:, d, h], root[:, d, h], ACT.Square, scale=root_tri[:, d, h : h + 1])
+            nc.vector.tensor_tensor(term[:, d, h0:h1], er_t[d][:, h0:h1], weight[:, d, h0:h1], ALU.mult)
             for total, part in ((den, weight), (num, term)):
-                for h in range(H):
-                    nc.tensor.matmul(total[h][:], part[:, h, :], ident[:], start=(d == 0), stop=(d == D - 1), is_transpose=True)
+                for h in range(h0, h1):
+                    nc.tensor.matmul(total[h][:], part[:, d, h], ident[:], start=(d == 0), stop=(d == D - 1), is_transpose=True)
 
         res = row("res", V)
         r_den = [row("r_den%d" % h, P) for h in range(H)]

@@ -46,23 +46,23 @@ def tile_picked_yddgi_root_p_kernel(
         ident = row("ident", P)
         tri_rows, dist_rows = row("tri_rows", P), row("dist_rows", P)
 
-        nc.gpsimd.memset(s_tab[:].bitcast(I32), 0)
-        for q in range(4):
-            nc.gpsimd.dma_start(s_tab[32 * q : 32 * q + 4 * PASSES, :].bitcast(I32), x_scales[:, 4 * q : 4 * q + 4, :].bitcast(I32))
+        nc.vector.memset(s_tab[:].bitcast(I32), 0)
         make_identity(nc, ident[:])
 
         nc.sync.dma_start(offs_t[:], offs)
         nc.sync.dma_start(x_tab[0][:].bitcast(I32), x_words[0].rearrange("p n t -> p (n t)").bitcast(I32))
+        for q in range(4):
+            nc.sync.dma_start(s_tab[32 * q : 32 * q + 4 * PASSES, :].bitcast(I32), x_scales[:, 4 * q : 4 * q + 4, :].bitcast(I32))
 
         def load_weights(i, o):
             rows = (w1, w2, w3)[i][o * P * PACK : (o + 1) * P * PACK, :]
             nc.sync.dma_start(w_raw[i][o][:], rows.rearrange("(p t) m -> p t m", t=PACK))
 
-        for i in range(3):
+        for i in range(2):
             load_weights(i, 0)
         nc.sync.dma_start(x_tab[1][:].bitcast(I32), x_words[1].rearrange("p n t -> p (n t)").bitcast(I32))
-        for i in range(3):
-            load_weights(i, 1)
+        for i, o in ((0, 1), (1, 1), (2, 0), (2, 1)):
+            load_weights(i, o)
         for d, pos in enumerate((pos1, pos2, pos3, pos4)):
             nc.sync.dma_start(pos_t[d][:], pos)
         for rows, src in ((tri_rows, tri), (dist_rows, dist)):
@@ -74,31 +74,43 @@ def tile_picked_yddgi_root_p_kernel(
         nc.vector.tensor_copy(s_pick[:], s_tab[:].indirect(offs_t[:]))
         nc.vector.tensor_copy(x_pick[1][:], x_tab[1][:].indirect(offs_t[:]))
 
-        acc = [bank("product%d" % i, i, [P, S]) for i in range(3)]
+        irr, mean = bank("irr", 0, [P, S]), bank("mean", 1, [P, S])
+        msq = [bank("msq%d" % a, (2, 5)[a], [P, S // 2]) for a in range(2)]
+        halves = [slice(a * S // 2, (a + 1) * S // 2) for a in range(2)]
+        targets = [[(irr, slice(0, S))], [(mean, slice(0, S))], list(zip(msq, halves))]
+        def quantise(i, o):
+            w_bf = held.tile([P, M, PACK], BF16, name="w_bf%d_%d" % (i, o), align_bytes=64)
+            w_codes = held.tile([P, M], U32, name="w_codes%d_%d" % (i, o), align_bytes=64)
+            w_scales = held.tile([P, M], U8, name="w_scales%d_%d" % (i, o), align_bytes=64)
+            src = w_raw[i][o][:].rearrange("p t m -> p m t")
+            if (i, o) != (2, 1):
+                nc.scalar.copy(w_bf[:], src)
+            else:
+                nc.vector.tensor_copy(w_bf[:], src)
+            nc.vector.quantize_mx(
+                out=w_codes[:].bitcast(FP8X4), scales=w_scales[:], in_=w_bf[:].rearrange("p m t -> p (m t)")
+            )
+            return w_codes, w_scales
+
+        def multiply(product, picked, o, quantised):
+            w_codes, w_scales = quantised
+            nc.tensor.matmul_mx(
+                out=product[:],
+                lhsT=w_codes[:].bitcast(FP8X4),
+                lhsT_scale=w_scales[:],
+                rhs=x_pick[o][:, picked].bitcast(FP8X4),
+                rhs_scale=s_pick[4 * o : P, picked],
+                start=(o == 0),
+                stop=(o == PASSES - 1),
+            )
+
         for o in range(PASSES):
-            for i in range(3):
-                product = acc[i]
-                w_bf = held.tile([P, M, PACK], BF16, name="w_bf%d_%d" % (i, o), align_bytes=64)
-                w_codes = held.tile([P, M], U32, name="w_codes%d_%d" % (i, o), align_bytes=64)
-                w_scales = held.tile([P, M], U8, name="w_scales%d_%d" % (i, o), align_bytes=64)
-                src = w_raw[i][o][:].rearrange("p t m -> p m t")
-                if (i, o) != (2, 1):
-                    nc.scalar.copy(w_bf[:], src)
-                else:
-                    nc.vector.tensor_copy(w_bf[:], src)
-                nc.vector.quantize_mx(
-                    out=w_codes[:].bitcast(FP8X4), scales=w_scales[:], in_=w_bf[:].rearrange("p m t -> p (m t)")
-                )
-                nc.tensor.matmul_mx(
-                    out=product[:],
-                    lhsT=w_codes[:].bitcast(FP8X4),
-                    lhsT_scale=w_scales[:],
-                    rhs=x_pick[o][:].bitcast(FP8X4),
-                    rhs_scale=s_pick[4 * o : P, :],
-                    start=(o == 0),
-                    stop=(o == PASSES - 1),
-                )
-        irr, mean, msq = acc
+            for i, product in enumerate((irr, mean)):
+                multiply(product, slice(0, S), o, quantise(i, o))
+        w3_passes = [quantise(2, o) for o in range(PASSES)]
+        for product, picked in targets[2]:
+            for o in range(PASSES):
+                multiply(product, picked, o, w3_passes[o])
 
         def fetch_turned(picked, window, d, dst):
             nc.vector.tensor_copy(picked, window[:].indirect(pos_t[d][:]))
@@ -110,7 +122,8 @@ def tile_picked_yddgi_root_p_kernel(
         capped = held.tile([P, 2, S], F32, name="capped")
         nc.scalar.activation(er[:], irr[:], ACT.Exp, scale=0.5)
         nc.scalar.activation(grown[:, 0, :], mean[:], ACT.Exp)
-        nc.scalar.activation(grown[:, 1, :], msq[:], ACT.Exp)
+        for product, picked in targets[2]:
+            nc.scalar.activation(grown[:, 1, picked], product[:], ACT.Exp)
         nc.vector.tensor_scalar(capped[:], grown[:], EXP_CAP, None, ALU.min)
 
         turned = bank("turned", 7, [P, 2, D, P // D])
@@ -133,7 +146,8 @@ def tile_picked_yddgi_root_p_kernel(
         nc.scalar.activation(log_mean[:], capped[:, 0, :], ACT.Ln, bias=1.0)
         nc.scalar.activation(log_msq[:], capped[:, 1, :], ACT.Ln, bias=1.0)
         nc.vector.tensor_tensor(mu[:], mean[:], log_mean[:], ALU.max)
-        nc.vector.tensor_tensor(sq[:], msq[:], log_msq[:], ALU.max)
+        for product, picked in targets[2]:
+            nc.vector.tensor_tensor(sq[:, picked], product[:], log_msq[:, picked], ALU.max)
 
         mu2, diff, spread, rstd = row("mu2"), row("diff"), row("spread"), row("rstd")
         nc.vector.tensor_tensor(mu2[:], mu[:], mu[:], ALU.mult)

@@ -152,7 +152,7 @@ def tile_picked_yddgi_root_p_kernel(
         mu2, diff, spread, rstd = row("mu2"), row("diff"), row("spread"), row("rstd")
         nc.vector.tensor_tensor(mu2[:], mu[:], mu[:], ALU.mult)
         r_tri = held.tile([P, D, H], F32, name="r_tri", tag="log_mean")
-        root_tri = held.tile([P, D, H], F32, name="root_tri")
+        root_tri = held.tile([P, D, H], F32, name="root_tri", tag="sq")
         nc.scalar.activation(r_tri[:], tri_col, ACT.Abs_reciprocal_sqrt, bias=TINY)
         nc.vector.tensor_tensor(diff[:], mu2[:], sq[:], ALU.subtract)
         nc.scalar.activation(spread[:], diff[:], ACT.Abs)
@@ -164,11 +164,12 @@ def tile_picked_yddgi_root_p_kernel(
         mu_picks = held.tile([P, D, V], F32, name="mu_picks", tag="mu2")
         mu_pick = [mu_picks[:, d, :] for d in range(D)]
         first_gap = held.tile([P, H, P], F32, name="first_gap", tag="spread")
-        later_gaps = held.tile([P, D - 1, H, P], F32, name="later_gaps", tag="rstd")
-        gap = [first_gap[:]] + [later_gaps[:, d] for d in range(D - 1)]
+        middle_gaps = held.tile([P, 2, H, P], F32, name="middle_gaps", tag="rstd")
+        last_gap = held.tile([P, H, P], F32, name="last_gap")
+        gap = [first_gap[:], middle_gaps[:, 0], middle_gaps[:, 1], last_gap[:]]
         gap_sq = [held.tile([P, H, P], F32, name="gap_sq%d" % d) for d in range(D)]
         for d in range(D):
-            mu_t = bank("mu_t%d" % d, (5, 6, 1, 2)[d], [P, H, P])
+            mu_t = bank("mu_t%d" % d, (5, 6, 1, 6)[d], [P, H, P])
             fetch_turned(mu_pick[d], mu, d, mu_t)
             for h in range(H):
                 nc.scalar.activation(gap[d][:, h, :], mu_t[:, h, :], ACT.Relu, scale=-1.0, bias=dist_col[:, d, h : h + 1])
@@ -177,16 +178,13 @@ def tile_picked_yddgi_root_p_kernel(
         nc.scalar.activation(gap_sq[D - 1][:], gap[D - 1], ACT.Square)
 
         steps = [(d, 0, H) for d in range(D - 1)] + [(D - 1, h, h + 1) for h in range(H)]
-        root = held.tile([P, D, H, P], F32, name="root", tag="rstd")
         ratio = held.tile([P, D, H, P], F32, name="ratio")
-        weight = held.tile([P, D, H, P], F32, name="weight")
-        term = held.tile([P, D, H, P], F32, name="term", tag="gap_sq%d" % (D - 1))
         inv_t = []
 
         def fetch_inv_var(s):
             d, h0, h1 = steps[s]
             picked = held.tile([P, h1 - h0, P], F32, name="inv_pick%d" % s)
-            dst = bank("inv_t%d" % s, (0, 7, 5, 6, 1)[s], [P, h1 - h0, P])
+            dst = bank("inv_t%d" % s, (0, 7, 5, 2, 1)[s], [P, h1 - h0, P])
             cols16 = P // 16
             nc.vector.tensor_copy(
                 picked[:].rearrange("p h v -> p (h v)"), inv_var[:].indirect(pos_t[d][:, h0 * cols16 : h1 * cols16])
@@ -195,25 +193,44 @@ def tile_picked_yddgi_root_p_kernel(
                 nc.tensor.transpose(dst[:, h, :], picked[:, h, :], ident[:])
             inv_t.append(dst)
 
-        for s in range(len(steps)):
-            fetch_inv_var(s)
-        for s, (d, h0, h1) in enumerate(steps):
+        def make_ratio(s):
+            d, h0, h1 = steps[s]
             nc.vector.tensor_tensor(ratio[:, d, h0:h1], inv_t[s][:], gap_sq[d][:, h0:h1], ALU.mult)
-        den = [bank("den%d" % h, (2, 0)[h], [P, P]) for h in range(H)]
-        num = [bank("num%d" % h, (7, 5)[h], [P, P]) for h in range(H)]
-        for d, h0, h1 in steps:
-            nc.scalar.activation(root[:, d, h0:h1], ratio[:, d, h0:h1], ACT.Abs_reciprocal_sqrt, bias=1.0)
+
+        def add_probe(s, root, weight, term):
+            d, h0, h1 = steps[s]
+            nc.scalar.activation(root[:, h0:h1], ratio[:, d, h0:h1], ACT.Abs_reciprocal_sqrt, bias=1.0)
             for h in range(h0, h1):
                 if d % 2 == 0:
                     nc.vector.scalar_tensor_tensor(
-                        weight[:, d, h], root[:, d, h], tri_col[:, d, h : h + 1], root[:, d, h], ALU.mult, ALU.mult
+                        weight[:, h], root[:, h], tri_col[:, d, h : h + 1], root[:, h], ALU.mult, ALU.mult
                     )
                 else:
-                    nc.scalar.activation(weight[:, d, h], root[:, d, h], ACT.Square, scale=root_tri[:, d, h : h + 1])
-            nc.vector.tensor_tensor(term[:, d, h0:h1], er_t[d][:, h0:h1], weight[:, d, h0:h1], ALU.mult)
-            for total, part in ((den, weight), (num, term)):
+                    nc.scalar.activation(weight[:, h], root[:, h], ACT.Square, scale=root_tri[:, d, h : h + 1])
+            nc.vector.tensor_tensor(term[:, h0:h1], er_t[d][:, h0:h1], weight[:, h0:h1], ALU.mult)
+            for total, addend in ((den, weight), (num, term)):
                 for h in range(h0, h1):
-                    nc.tensor.matmul(total[h][:], part[:, d, h], ident[:], start=(d == 0), stop=(d == D - 1), is_transpose=True)
+                    nc.tensor.matmul(total[h][:], addend[:, h], ident[:], start=(d == 0), stop=(d == D - 1), is_transpose=True)
+
+        for s in range(len(steps)):
+            fetch_inv_var(s)
+        make_ratio(0)
+        make_ratio(1)
+        den = [bank("den%d" % h, (0, 6)[h], [P, P]) for h in range(H)]
+        first_root = held.tile([P, H, P], F32, name="first_root", tag="rstd")
+        first_weight = held.tile([P, H, P], F32, name="first_weight", tag="inv_var")
+        first_term = held.tile([P, H, P], F32, name="first_term")
+        make_ratio(2)
+        num = [bank("num%d" % h, (7, 5)[h], [P, P]) for h in range(H)]
+        add_probe(0, first_root[:], first_weight[:], first_term[:])
+        for s in range(3, len(steps)):
+            make_ratio(s)
+        roots = held.tile([P, D - 1, H, P], F32, name="roots", tag="last_gap")
+        weights = held.tile([P, D - 1, H, P], F32, name="weights")
+        terms = held.tile([P, D - 1, H, P], F32, name="terms", tag="gap_sq%d" % (D - 1))
+        for s in range(1, len(steps)):
+            d = steps[s][0]
+            add_probe(s, roots[:, d - 1], weights[:, d - 1], terms[:, d - 1])
 
         res = row("res", V)
         r_den = [row("r_den%d" % h, P) for h in range(H)]

@@ -19,9 +19,13 @@ ACT = mybir.ActivationFunctionType
 P = 128
 PACK = 4
 PASSES = K // (P * PACK)
-EXP_CAP = 2.0 ** 60
-TINY = 1e-30
+QUADRANTS = 4
+SCALE_ROWS = 4
+GROUP = 16
 H = V // P
+EXP_CAP = 2.0**60
+TINY = 1e-30
+IRR, MEAN, MSQ = 0, 1, 2
 
 
 def tile_picked_yddgi_root_p_kernel(
@@ -38,35 +42,41 @@ def tile_picked_yddgi_root_p_kernel(
         def bank(name, b, shape):
             return psum.tile(shape, F32, name=name, tag="bank%d" % b)
 
-        offs_t = held.tile([P, S // 16], U16, name="offs_t")
-        pos_t = [held.tile([P, V // 16], U16, name="pos_t%d" % d) for d in range(D)]
+        offs_t = held.tile([P, S // GROUP], U16, name="offs_t")
+        pos_t = [held.tile([P, V // GROUP], U16, name="pos_t%d" % d) for d in range(D)]
         x_tab = [held.tile([P, T], U32, name="x_tab%d" % o) for o in range(PASSES)]
         s_tab = held.tile([P, T], U8, name="s_tab")
         w_raw = [[held.tile([P, PACK, M], F32, name="w_raw%d_%d" % (i, o)) for o in range(PASSES)] for i in range(3)]
         ident = row("ident", P)
-        tri_rows, dist_rows = row("tri_rows", P), row("dist_rows", P)
+        point_rows = row("point_rows", P)
 
         nc.vector.memset(s_tab[:].bitcast(I32), 0)
         make_identity(nc, ident[:])
+        nc.gpsimd.memset(point_rows[:], 0.0)
 
-        nc.sync.dma_start(offs_t[:], offs)
-        nc.sync.dma_start(x_tab[0][:].bitcast(I32), x_words[0].rearrange("p n t -> p (n t)").bitcast(I32))
-        for q in range(4):
-            nc.sync.dma_start(s_tab[32 * q : 32 * q + 4 * PASSES, :].bitcast(I32), x_scales[:, 4 * q : 4 * q + 4, :].bitcast(I32))
+        def load_words(o):
+            nc.sync.dma_start(x_tab[o][:].bitcast(I32), x_words[o].rearrange("p n t -> p (n t)").bitcast(I32))
 
         def load_weights(i, o):
             rows = (w1, w2, w3)[i][o * P * PACK : (o + 1) * P * PACK, :]
             nc.sync.dma_start(w_raw[i][o][:], rows.rearrange("(p t) m -> p t m", t=PACK))
 
-        for i in range(2):
-            load_weights(i, 0)
-        nc.sync.dma_start(x_tab[1][:].bitcast(I32), x_words[1].rearrange("p n t -> p (n t)").bitcast(I32))
-        for i, o in ((0, 1), (1, 1), (2, 0), (2, 1)):
+        nc.sync.dma_start(offs_t[:], offs)
+        load_words(0)
+        for q in range(QUADRANTS):
+            nc.sync.dma_start(
+                s_tab[32 * q : 32 * q + SCALE_ROWS * PASSES, :].bitcast(I32),
+                x_scales[:, SCALE_ROWS * q : SCALE_ROWS * (q + 1), :].bitcast(I32),
+            )
+        load_weights(IRR, 0)
+        load_weights(MEAN, 0)
+        load_words(1)
+        for i, o in ((IRR, 1), (MEAN, 1), (MSQ, 0), (MSQ, 1)):
             load_weights(i, o)
         for d, pos in enumerate((pos1, pos2, pos3, pos4)):
             nc.sync.dma_start(pos_t[d][:], pos)
-        for rows, src in ((tri_rows, tri), (dist_rows, dist)):
-            nc.sync.dma_start(rows[:], src[:, 0 : P // (D * H), :].rearrange("d r (h v) -> d (r h) v", h=H))
+        for a, src in enumerate((tri, dist)):
+            nc.sync.dma_start(point_rows[a * D * H : (a + 1) * D * H, :], src[:, 0, :].rearrange("d (h v) -> d h v", h=H))
 
         x_pick = [held.tile([P, S], U32, name="x_pick%d" % o, align_bytes=64) for o in range(PASSES)]
         s_pick = held.tile([P, S], U8, name="s_pick", align_bytes=64)
@@ -77,40 +87,40 @@ def tile_picked_yddgi_root_p_kernel(
         irr, mean = bank("irr", 0, [P, S]), bank("mean", 1, [P, S])
         msq = [bank("msq%d" % a, (2, 5)[a], [P, S // 2]) for a in range(2)]
         halves = [slice(a * S // 2, (a + 1) * S // 2) for a in range(2)]
-        targets = [[(irr, slice(0, S))], [(mean, slice(0, S))], list(zip(msq, halves))]
+
         def quantise(i, o):
             w_bf = held.tile([P, M, PACK], BF16, name="w_bf%d_%d" % (i, o), align_bytes=64)
             w_codes = held.tile([P, M], U32, name="w_codes%d_%d" % (i, o), align_bytes=64)
             w_scales = held.tile([P, M], U8, name="w_scales%d_%d" % (i, o), align_bytes=64)
             src = w_raw[i][o][:].rearrange("p t m -> p m t")
-            if (i, o) != (2, 1):
-                nc.scalar.copy(w_bf[:], src)
-            else:
+            if (i, o) == (MSQ, PASSES - 1):
                 nc.vector.tensor_copy(w_bf[:], src)
+            else:
+                nc.scalar.copy(w_bf[:], src)
             nc.vector.quantize_mx(
                 out=w_codes[:].bitcast(FP8X4), scales=w_scales[:], in_=w_bf[:].rearrange("p m t -> p (m t)")
             )
             return w_codes, w_scales
 
-        def multiply(product, picked, o, quantised):
+        def multiply(product, texels, o, quantised):
             w_codes, w_scales = quantised
             nc.tensor.matmul_mx(
                 out=product[:],
                 lhsT=w_codes[:].bitcast(FP8X4),
                 lhsT_scale=w_scales[:],
-                rhs=x_pick[o][:, picked].bitcast(FP8X4),
-                rhs_scale=s_pick[4 * o : P, picked],
+                rhs=x_pick[o][:, texels].bitcast(FP8X4),
+                rhs_scale=s_pick[SCALE_ROWS * o : P, texels],
                 start=(o == 0),
                 stop=(o == PASSES - 1),
             )
 
         for o in range(PASSES):
-            for i, product in enumerate((irr, mean)):
+            for i, product in ((IRR, irr), (MEAN, mean)):
                 multiply(product, slice(0, S), o, quantise(i, o))
-        w3_passes = [quantise(2, o) for o in range(PASSES)]
-        for product, picked in targets[2]:
+        w3_passes = [quantise(MSQ, o) for o in range(PASSES)]
+        for product, half in zip(msq, halves):
             for o in range(PASSES):
-                multiply(product, picked, o, w3_passes[o])
+                multiply(product, half, o, w3_passes[o])
 
         def fetch_turned(picked, window, d, dst):
             nc.vector.tensor_copy(picked, window[:].indirect(pos_t[d][:]))
@@ -122,47 +132,47 @@ def tile_picked_yddgi_root_p_kernel(
         capped = held.tile([P, 2, S], F32, name="capped")
         nc.scalar.activation(er[:], irr[:], ACT.Exp, scale=0.5)
         nc.scalar.activation(grown[:, 0, :], mean[:], ACT.Exp)
-        for product, picked in targets[2]:
-            nc.scalar.activation(grown[:, 1, picked], product[:], ACT.Exp)
+        for product, half in zip(msq, halves):
+            nc.scalar.activation(grown[:, 1, half], product[:], ACT.Exp)
         nc.vector.tensor_scalar(capped[:], grown[:], EXP_CAP, None, ALU.min)
 
-        turned = bank("turned", 7, [P, 2, D, P // D])
-        nc.tensor.transpose(turned[:, 0].rearrange("p d c -> p (d c)"), tri_rows[:], ident[:])
-        nc.tensor.transpose(turned[:, 1].rearrange("p d c -> p (d c)"), dist_rows[:], ident[:])
+        turned = bank("turned", 7, [P, P])
+        nc.tensor.transpose(turned[:], point_rows[:], ident[:])
         cols = held.tile([P, 2, D, H], F32, name="cols")
-        nc.vector.tensor_copy(cols[:], turned[:, :, :, 0:H])
+        nc.vector.tensor_copy(cols[:].rearrange("p a d h -> p (a d h)"), turned[:, 0 : 2 * D * H])
         tri_col, dist_col = cols[:, 0], cols[:, 1]
 
         er_pair = [bank("er_pair%d" % a, 3 + a, [P, 2, H, P]) for a in range(D // 2)]
         er_t = [er_pair[d // 2][:, d % 2] for d in range(D)]
-        er_pick = [
-            held.tile([P, D - 1, V], F32, name="er_early", tag="w_bf2_1", align_bytes=64),
-            held.tile([P, 1, V], F32, name="er_late", tag="grown"),
-        ]
+        er_early = held.tile([P, D - 1, V], F32, name="er_early", tag="w_bf%d_%d" % (MSQ, PASSES - 1), align_bytes=64)
+        er_late = held.tile([P, 1, V], F32, name="er_late", tag="grown")
+        er_pick = [er_early[:, d, :] for d in range(D - 1)] + [er_late[:, 0, :]]
         for d in range(D):
-            fetch_turned(er_pick[d // (D - 1)][:, d % (D - 1), :], er, d, er_t[d])
+            fetch_turned(er_pick[d], er, d, er_t[d])
 
         log_mean, log_msq, mu, sq = row("log_mean"), row("log_msq"), row("mu"), row("sq")
         nc.scalar.activation(log_mean[:], capped[:, 0, :], ACT.Ln, bias=1.0)
         nc.scalar.activation(log_msq[:], capped[:, 1, :], ACT.Ln, bias=1.0)
         nc.vector.tensor_tensor(mu[:], mean[:], log_mean[:], ALU.max)
-        for product, picked in targets[2]:
-            nc.vector.tensor_tensor(sq[:, picked], product[:], log_msq[:, picked], ALU.max)
-
         mu2, diff, spread, rstd = row("mu2"), row("diff"), row("spread"), row("rstd")
-        nc.vector.tensor_tensor(mu2[:], mu[:], mu[:], ALU.mult)
+        inv_var = row("inv_var")
         r_tri = held.tile([P, D, H], F32, name="r_tri", tag="log_mean")
         root_tri = held.tile([P, D, H], F32, name="root_tri", tag="sq")
         nc.scalar.activation(r_tri[:], tri_col, ACT.Abs_reciprocal_sqrt, bias=TINY)
-        nc.vector.tensor_tensor(diff[:], mu2[:], sq[:], ALU.subtract)
-        nc.scalar.activation(spread[:], diff[:], ACT.Abs)
-        nc.scalar.activation(rstd[:], spread[:], ACT.Abs_reciprocal_sqrt, bias=0.05)
-        inv_var = row("inv_var")
-        nc.scalar.activation(inv_var[:], rstd[:], ACT.Square)
+        nc.vector.tensor_tensor(sq[:, halves[0]], msq[0][:], log_msq[:, halves[0]], ALU.max)
+        nc.vector.tensor_tensor(mu2[:], mu[:], mu[:], ALU.mult)
+        nc.vector.tensor_tensor(sq[:, halves[1]], msq[1][:], log_msq[:, halves[1]], ALU.max)
+        for half in halves:
+            nc.vector.tensor_tensor(diff[:, half], mu2[:, half], sq[:, half], ALU.subtract)
+        for half in halves:
+            nc.scalar.activation(spread[:, half], diff[:, half], ACT.Abs)
+        for half in halves:
+            nc.scalar.activation(rstd[:, half], spread[:, half], ACT.Abs_reciprocal_sqrt, bias=0.05)
+        for half in halves:
+            nc.scalar.activation(inv_var[:, half], rstd[:, half], ACT.Square)
         nc.vector.tensor_tensor(root_tri[:], tri_col, r_tri[:], ALU.mult)
 
         mu_picks = held.tile([P, D, V], F32, name="mu_picks", tag="mu2")
-        mu_pick = [mu_picks[:, d, :] for d in range(D)]
         first_gap = held.tile([P, H, P], F32, name="first_gap", tag="spread")
         middle_gaps = held.tile([P, 2, H, P], F32, name="middle_gaps", tag="rstd")
         last_gap = held.tile([P, H, P], F32, name="last_gap")
@@ -170,7 +180,7 @@ def tile_picked_yddgi_root_p_kernel(
         gap_sq = [held.tile([P, H, P], F32, name="gap_sq%d" % d) for d in range(D)]
         for d in range(D):
             mu_t = bank("mu_t%d" % d, (5, 6, 1, 6)[d], [P, H, P])
-            fetch_turned(mu_pick[d], mu, d, mu_t)
+            fetch_turned(mu_picks[:, d, :], mu, d, mu_t)
             for h in range(H):
                 nc.scalar.activation(gap[d][:, h, :], mu_t[:, h, :], ACT.Relu, scale=-1.0, bias=dist_col[:, d, h : h + 1])
             if d > 0:
@@ -185,10 +195,8 @@ def tile_picked_yddgi_root_p_kernel(
             d, h0, h1 = steps[s]
             picked = held.tile([P, h1 - h0, P], F32, name="inv_pick%d" % s)
             dst = bank("inv_t%d" % s, (0, 7, 5, 2, 1)[s], [P, h1 - h0, P])
-            cols16 = P // 16
-            nc.vector.tensor_copy(
-                picked[:].rearrange("p h v -> p (h v)"), inv_var[:].indirect(pos_t[d][:, h0 * cols16 : h1 * cols16])
-            )
+            entries = pos_t[d][:, h0 * P // GROUP : h1 * P // GROUP]
+            nc.vector.tensor_copy(picked[:].rearrange("p h v -> p (h v)"), inv_var[:].indirect(entries))
             for h in range(h1 - h0):
                 nc.tensor.transpose(dst[:, h, :], picked[:, h, :], ident[:])
             inv_t.append(dst)
@@ -223,7 +231,7 @@ def tile_picked_yddgi_root_p_kernel(
         make_ratio(2)
         num = [bank("num%d" % h, (7, 5)[h], [P, P]) for h in range(H)]
         add_probe(0, first_root[:], first_weight[:], first_term[:])
-        for s in range(3, len(steps)):
+        for s in range(D - 1, len(steps)):
             make_ratio(s)
         roots = held.tile([P, D - 1, H, P], F32, name="roots", tag="last_gap")
         weights = held.tile([P, D - 1, H, P], F32, name="weights")
@@ -236,12 +244,12 @@ def tile_picked_yddgi_root_p_kernel(
         r_den = [row("r_den%d" % h, P) for h in range(H)]
         for h in range(H):
             nc.scalar.activation(r_den[h][:], den[h][:], ACT.Abs_reciprocal_sqrt, bias=0.02)
+        scaled_num, r_num = [], []
         for h in range(H):
-            r_num, part = row("r_num%d" % h, P), row("part%d" % h, P)
-            if h == 0:
-                nc.vector.tensor_tensor(part[:], num[h][:], r_den[h][:], ALU.mult)
-            nc.scalar.activation(r_num[:], num[h][:], ACT.Abs_reciprocal_sqrt, bias=TINY)
-            if h == 1:
-                nc.vector.tensor_tensor(part[:], num[h][:], r_den[h][:], ALU.mult)
-            nc.vector.tensor_tensor(res[:, h * P : (h + 1) * P], part[:], r_num[:], ALU.mult)
+            r_num.append(row("r_num%d" % h, P))
+            scaled_num.append(row("scaled_num%d" % h, P))
+            nc.scalar.activation(r_num[h][:], num[h][:], ACT.Abs_reciprocal_sqrt, bias=TINY)
+            nc.vector.tensor_tensor(scaled_num[h][:], num[h][:], r_den[h][:], ALU.mult)
+        for h in range(H):
+            nc.vector.tensor_tensor(res[:, h * P : (h + 1) * P], scaled_num[h][:], r_num[h][:], ALU.mult)
         nc.sync.dma_start(out, res[:])

from contextlib import ExitStack

import concourse.mybir as mybir
from concourse.masks import make_identity

K, T, S, M, D, V = 1024, 2048, 512, 128, 4, 256
FLOPS = 3 * 2 * K * M * S

F32 = mybir.dt.float32
BF16 = mybir.dt.bfloat16
I32 = mybir.dt.int32
U32 = mybir.dt.uint32
U16 = mybir.dt.uint16
U8 = mybir.dt.uint8
FP8X4 = mybir.dt.float8_e4m3fn_x4
ALU = mybir.AluOpType
ACT = mybir.ActivationFunctionType

P = 128
PACK = 4
PASSES = K // (P * PACK)
QUADRANTS = 4
SCALE_ROWS = 4
GROUP = 16
H = V // P
EXP_CAP = 2.0**60
TINY = 1e-30
IRR, MEAN, MSQ = 0, 1, 2


def tile_picked_yddgi_root_p_kernel(
    tc, x_words, x_scales, w1, w2, w3, tri, dist, offs, pos1, pos2, pos3, pos4, out
):
    nc = tc.nc
    with ExitStack() as ctx:
        held = ctx.enter_context(tc.tile_pool(name="held", bufs=1))
        psum = ctx.enter_context(tc.psum_pool(name="psum", bufs=1))

        def row(name, width=S):
            return held.tile([P, width], F32, name=name)

        def bank(name, b, shape):
            return psum.tile(shape, F32, name=name, tag="bank%d" % b)

        offs_t = held.tile([P, S // GROUP], U16, name="offs_t")
        pos_t = [held.tile([P, V // GROUP], U16, name="pos_t%d" % d) for d in range(D)]
        x_tab = [held.tile([P, T], U32, name="x_tab%d" % o) for o in range(PASSES)]
        s_tab = held.tile([P, T], U8, name="s_tab")
        w_raw = [[held.tile([P, PACK, M], F32, name="w_raw%d_%d" % (i, o)) for o in range(PASSES)] for i in range(3)]
        ident = row("ident", P)
        point_rows = row("point_rows", P)

        nc.vector.memset(s_tab[:].bitcast(I32), 0)
        make_identity(nc, ident[:])
        nc.gpsimd.memset(point_rows[:], 0.0)

        def load_words(o):
            nc.sync.dma_start(x_tab[o][:].bitcast(I32), x_words[o].rearrange("p n t -> p (n t)").bitcast(I32))

        def load_weights(i, o):
            rows = (w1, w2, w3)[i][o * P * PACK : (o + 1) * P * PACK, :]
            nc.sync.dma_start(w_raw[i][o][:], rows.rearrange("(p t) m -> p t m", t=PACK))

        nc.sync.dma_start(offs_t[:], offs)
        load_words(0)
        for q in range(QUADRANTS):
            nc.sync.dma_start(
                s_tab[32 * q : 32 * q + SCALE_ROWS * PASSES, :].bitcast(I32),
                x_scales[:, SCALE_ROWS * q : SCALE_ROWS * (q + 1), :].bitcast(I32),
            )
        load_weights(IRR, 0)
        load_weights(MEAN, 0)
        load_words(1)
        for i, o in ((IRR, 1), (MEAN, 1), (MSQ, 0), (MSQ, 1)):
            load_weights(i, o)
        for d, pos in enumerate((pos1, pos2, pos3, pos4)):
            nc.sync.dma_start(pos_t[d][:], pos)
        for a, src in enumerate((tri, dist)):
            nc.sync.dma_start(point_rows[a * D * H : (a + 1) * D * H, :], src[:, 0, :].rearrange("d (h v) -> d h v", h=H))

        x_pick = [held.tile([P, S], U32, name="x_pick%d" % o, align_bytes=64) for o in range(PASSES)]
        s_pick = held.tile([P, S], U8, name="s_pick", align_bytes=64)
        nc.vector.tensor_copy(x_pick[0][:], x_tab[0][:].indirect(offs_t[:]))
        nc.vector.tensor_copy(s_pick[:], s_tab[:].indirect(offs_t[:]))
        nc.vector.tensor_copy(x_pick[1][:], x_tab[1][:].indirect(offs_t[:]))

        irr, mean = bank("irr", 0, [P, S]), bank("mean", 1, [P, S])
        msq = [bank("msq%d" % a, (2, 5)[a], [P, S // 2]) for a in range(2)]
        halves = [slice(a * S // 2, (a + 1) * S // 2) for a in range(2)]

        def quantise(i, o):
            w_bf = held.tile([P, M, PACK], BF16, name="w_bf%d_%d" % (i, o), align_bytes=64)
            w_codes = held.tile([P, M], U32, name="w_codes%d_%d" % (i, o), align_bytes=64)
            w_scales = held.tile([P, M], U8, name="w_scales%d_%d" % (i, o), align_bytes=64)
            src = w_raw[i][o][:].rearrange("p t m -> p m t")
            if (i, o) == (MSQ, PASSES - 1):
                nc.vector.tensor_copy(w_bf[:], src)
            else:
                nc.scalar.copy(w_bf[:], src)
            nc.vector.quantize_mx(
                out=w_codes[:].bitcast(FP8X4), scales=w_scales[:], in_=w_bf[:].rearrange("p m t -> p (m t)")
            )
            return w_codes, w_scales

        def multiply(product, texels, o, quantised):
            w_codes, w_scales = quantised
            nc.tensor.matmul_mx(
                out=product[:],
                lhsT=w_codes[:].bitcast(FP8X4),
                lhsT_scale=w_scales[:],
                rhs=x_pick[o][:, texels].bitcast(FP8X4),
                rhs_scale=s_pick[SCALE_ROWS * o : P, texels],
                start=(o == 0),
                stop=(o == PASSES - 1),
            )

        for o in range(PASSES):
            for i, product in ((IRR, irr), (MEAN, mean)):
                multiply(product, slice(0, S), o, quantise(i, o))
        w3_passes = [quantise(MSQ, o) for o in range(PASSES)]
        for product, half in zip(msq, halves):
            for o in range(PASSES):
                multiply(product, half, o, w3_passes[o])

        def fetch_turned(picked, window, d, dst):
            nc.vector.tensor_copy(picked, window[:].indirect(pos_t[d][:]))
            for h in range(H):
                nc.tensor.transpose(dst[:, h, :], picked[:, h * P : (h + 1) * P], ident[:])

        er = row("er")
        grown = held.tile([P, 2, S], F32, name="grown")
        capped = held.tile([P, 2, S], F32, name="capped")
        nc.scalar.activation(er[:], irr[:], ACT.Exp, scale=0.5)
        nc.scalar.activation(grown[:, 0, :], mean[:], ACT.Exp)
        for product, half in zip(msq, halves):
            nc.scalar.activation(grown[:, 1, half], product[:], ACT.Exp)
        nc.vector.tensor_scalar(capped[:], grown[:], EXP_CAP, None, ALU.min)

        turned = bank("turned", 7, [P, P])
        nc.tensor.transpose(turned[:], point_rows[:], ident[:])
        cols = held.tile([P, 2, D, H], F32, name="cols")
        nc.vector.tensor_copy(cols[:].rearrange("p a d h -> p (a d h)"), turned[:, 0 : 2 * D * H])
        tri_col, dist_col = cols[:, 0], cols[:, 1]

        er_pair = [bank("er_pair%d" % a, 3 + a, [P, 2, H, P]) for a in range(D // 2)]
        er_t = [er_pair[d // 2][:, d % 2] for d in range(D)]
        er_early = held.tile([P, D - 1, V], F32, name="er_early", tag="w_bf%d_%d" % (MSQ, PASSES - 1), align_bytes=64)
        er_late = held.tile([P, 1, V], F32, name="er_late", tag="grown")
        er_pick = [er_early[:, d, :] for d in range(D - 1)] + [er_late[:, 0, :]]
        for d in range(D):
            fetch_turned(er_pick[d], er, d, er_t[d])

        log_mean, log_msq, mu, sq = row("log_mean"), row("log_msq"), row("mu"), row("sq")
        nc.scalar.activation(log_mean[:], capped[:, 0, :], ACT.Ln, bias=1.0)
        nc.scalar.activation(log_msq[:], capped[:, 1, :], ACT.Ln, bias=1.0)
        nc.vector.tensor_tensor(mu[:], mean[:], log_mean[:], ALU.max)
        mu2, diff, spread, rstd = row("mu2"), row("diff"), row("spread"), row("rstd")
        inv_var = row("inv_var")
        r_tri = held.tile([P, D, H], F32, name="r_tri", tag="log_mean")
        root_tri = held.tile([P, D, H], F32, name="root_tri", tag="sq")
        nc.scalar.activation(r_tri[:], tri_col, ACT.Abs_reciprocal_sqrt, bias=TINY)
        nc.vector.tensor_tensor(sq[:, halves[0]], msq[0][:], log_msq[:, halves[0]], ALU.max)
        nc.vector.tensor_tensor(mu2[:], mu[:], mu[:], ALU.mult)
        nc.vector.tensor_tensor(sq[:, halves[1]], msq[1][:], log_msq[:, halves[1]], ALU.max)
        for half in halves:
            nc.vector.tensor_tensor(diff[:, half], mu2[:, half], sq[:, half], ALU.subtract)
        for half in halves:
            nc.scalar.activation(spread[:, half], diff[:, half], ACT.Abs)
        for half in halves:
            nc.scalar.activation(rstd[:, half], spread[:, half], ACT.Abs_reciprocal_sqrt, bias=0.05)
        for half in halves:
            nc.scalar.activation(inv_var[:, half], rstd[:, half], ACT.Square)
        nc.vector.tensor_tensor(root_tri[:], tri_col, r_tri[:], ALU.mult)

        mu_picks = held.tile([P, D, V], F32, name="mu_picks", tag="mu2")
        first_gap = held.tile([P, H, P], F32, name="first_gap", tag="spread")
        middle_gaps = held.tile([P, 2, H, P], F32, name="middle_gaps", tag="rstd")
        last_gap = held.tile([P, H, P], F32, name="last_gap")
        gap = [first_gap[:], middle_gaps[:, 0], middle_gaps[:, 1], last_gap[:]]
        gap_sq = [held.tile([P, H, P], F32, name="gap_sq%d" % d) for d in range(D)]
        for d in range(D):
            mu_t = bank("mu_t%d" % d, (5, 6, 1, 6)[d], [P, H, P])
            fetch_turned(mu_picks[:, d, :], mu, d, mu_t)
            for h in range(H):
                nc.scalar.activation(gap[d][:, h, :], mu_t[:, h, :], ACT.Relu, scale=-1.0, bias=dist_col[:, d, h : h + 1])
            if d > 0:
                nc.scalar.activation(gap_sq[d - 1][:], gap[d - 1], ACT.Square)
        nc.scalar.activation(gap_sq[D - 1][:], gap[D - 1], ACT.Square)

        steps = [(d, 0, H) for d in range(D - 1)] + [(D - 1, h, h + 1) for h in range(H)]
        ratio = held.tile([P, D, H, P], F32, name="ratio")
        inv_t = []

        def fetch_inv_var(s):
            d, h0, h1 = steps[s]
            picked = held.tile([P, h1 - h0, P], F32, name="inv_pick%d" % s)
            dst = bank("inv_t%d" % s, (0, 7, 5, 2, 1)[s], [P, h1 - h0, P])
            entries = pos_t[d][:, h0 * P // GROUP : h1 * P // GROUP]
            nc.vector.tensor_copy(picked[:].rearrange("p h v -> p (h v)"), inv_var[:].indirect(entries))
            for h in range(h1 - h0):
                nc.tensor.transpose(dst[:, h, :], picked[:, h, :], ident[:])
            inv_t.append(dst)

        def make_ratio(s):
            d, h0, h1 = steps[s]
            nc.vector.tensor_tensor(ratio[:, d, h0:h1], inv_t[s][:], gap_sq[d][:, h0:h1], ALU.mult)

        def add_probe(s, root, weight, term):
            d, h0, h1 = steps[s]
            nc.scalar.activation(root[:, h0:h1], ratio[:, d, h0:h1], ACT.Abs_reciprocal_sqrt, bias=1.0)
            for h in range(h0, h1):
                if d % 2 == 0:
                    nc.vector.scalar_tensor_tensor(
                        weight[:, h], root[:, h], tri_col[:, d, h : h + 1], root[:, h], ALU.mult, ALU.mult
                    )
                else:
                    nc.scalar.activation(weight[:, h], root[:, h], ACT.Square, scale=root_tri[:, d, h : h + 1])
            nc.vector.tensor_tensor(term[:, h0:h1], er_t[d][:, h0:h1], weight[:, h0:h1], ALU.mult)
            for total, addend in ((den, weight), (num, term)):
                for h in range(h0, h1):
                    nc.tensor.matmul(total[h][:], addend[:, h], ident[:], start=(d == 0), stop=(d == D - 1), is_transpose=True)

        for s in range(len(steps)):
            fetch_inv_var(s)
        make_ratio(0)
        make_ratio(1)
        den = [bank("den%d" % h, (0, 6)[h], [P, P]) for h in range(H)]
        first_root = held.tile([P, H, P], F32, name="first_root", tag="rstd")
        first_weight = held.tile([P, H, P], F32, name="first_weight", tag="inv_var")
        first_term = held.tile([P, H, P], F32, name="first_term")
        make_ratio(2)
        num = [bank("num%d" % h, (7, 5)[h], [P, P]) for h in range(H)]
        add_probe(0, first_root[:], first_weight[:], first_term[:])
        for s in range(D - 1, len(steps)):
            make_ratio(s)
        roots = held.tile([P, D - 1, H, P], F32, name="roots", tag="last_gap")
        weights = held.tile([P, D - 1, H, P], F32, name="weights")
        terms = held.tile([P, D - 1, H, P], F32, name="terms", tag="gap_sq%d" % (D - 1))
        for s in range(1, len(steps)):
            d = steps[s][0]
            add_probe(s, roots[:, d - 1], weights[:, d - 1], terms[:, d - 1])

        res = row("res", V)
        r_den = [row("r_den%d" % h, P) for h in range(H)]
        for h in range(H):
            nc.scalar.activation(r_den[h][:], den[h][:], ACT.Abs_reciprocal_sqrt, bias=0.02)
        scaled_num, r_num = [], []
        for h in range(H):
            r_num.append(row("r_num%d" % h, P))
            scaled_num.append(row("scaled_num%d" % h, P))
            nc.scalar.activation(r_num[h][:], num[h][:], ACT.Abs_reciprocal_sqrt, bias=TINY)
            nc.vector.tensor_tensor(scaled_num[h][:], num[h][:], r_den[h][:], ALU.mult)
        for h in range(H):
            nc.vector.tensor_tensor(res[:, h * P : (h + 1) * P], scaled_num[h][:], r_num[h][:], ALU.mult)
        nc.sync.dma_start(out, res[:])
